import numpy as np
import ml_dtypes

BF16 = ml_dtypes.bfloat16


def bf(x):
    return np.asarray(x, np.float32).astype(BF16)


def f32(x):
    return np.asarray(x, np.float32)


def f64(x):
    return np.asarray(x).astype(np.float64)


def striped(idx):
    return np.tile(idx.reshape(-1, 16).T, (8, 1))


S, K, M, N, B, Q = 512, 128, 128, 192, 2, 96


def setup_inputs():
    return {"base": bf(np.random.standard_normal((B, M, S))), "x": bf(np.random.standard_normal((K, N))), "w": bf(np.random.standard_normal((K, M)) / np.sqrt(K)), "b": f32(0.5 * np.random.standard_normal((M, 1))), "offs": striped(np.random.permutation(S)[:N])}


def reference(base, x, w, b, offs):
    idx = offs[:16].T.reshape(-1)
    z = f64(base).copy()
    for i in range(B):
        z[i][:, idx[i * Q : (i + 1) * Q]] = f64(w).T @ f64(x)[:, i * Q : (i + 1) * Q]
    return np.tanh(z + f64(b))

@@ -1,0 +1,67 @@
+import concourse.mybir as mybir
+from concourse.masks import make_identity
+
+BF16, F32, U16 = mybir.dt.bfloat16, mybir.dt.float32, mybir.dt.uint16
+TANH = mybir.ActivationFunctionType.Tanh
+
+P = 128
+SEQUENCES = 2
+TOKENS = 512
+ENTRIES = 192
+PIECE = ENTRIES // SEQUENCES
+PIECE_COLUMNS = PIECE // 16
+
+WARMING_MATMULS = 2
+
+FLOPS = 2 * P * P * ENTRIES
+
+
+def tile_scatter_matmul_kernel(tc, base, x, w, b, offs, out):
+    nc = tc.nc
+    with (
+        tc.tile_pool(name="held", bufs=1) as held,
+        tc.psum_pool(name="windows", bufs=1) as windows,
+    ):
+        base_tiles = [held.tile([P, TOKENS], BF16, name=f"base{i}") for i in range(SEQUENCES)]
+        nc.sync.dma_start(base_tiles[0][:], base[0])
+        nc.sync.dma_start(base_tiles[1][:], base[1])
+        offsets = held.tile([P, ENTRIES // 16], U16, name="offsets")
+        nc.sync.dma_start(offsets[:], offs)
+        weights = held.tile([P, P], BF16, name="weights")
+        nc.sync.dma_start(weights[:], w)
+        picked = held.tile([P, ENTRIES], BF16, name="picked")
+        nc.sync.dma_start(picked[:], x)
+        bias = held.tile([P, 1], F32, name="bias")
+        nc.sync.dma_start(bias[:], b)
+
+        zeros = held.tile([P, TOKENS], BF16, name="zeros")
+        nc.vector.memset(zeros[:], 0.0)
+        idle_product = windows.tile([P, TOKENS], F32, name="idle_product")
+        for turn in range(WARMING_MATMULS):
+            nc.tensor.matmul(idle_product[:], zeros[:, 0:P], zeros[:], start=True, stop=True)
+
+        warm = held.tile([P, 1], F32, name="warm")
+        nc.vector.memset(warm[:], 0.0)
+        nc.scalar.activation(warm[:], warm[:], TANH)
+
+        identity = held.tile([P, P], BF16, name="identity")
+        make_identity(nc, identity[:])
+
+        window_tiles = [windows.tile([P, TOKENS], F32, name=f"window{i}") for i in range(SEQUENCES)]
+        for i in range(SEQUENCES):
+            nc.tensor.matmul(window_tiles[i][:], identity[:], base_tiles[i][:], start=True, stop=True)
+
+        for i in range(SEQUENCES):
+            piece = offsets[:, i * PIECE_COLUMNS : (i + 1) * PIECE_COLUMNS]
+            nc.tensor.matmul(
+                window_tiles[i][:].indirect(piece),
+                weights[:],
+                picked[:, i * PIECE : (i + 1) * PIECE],
+                start=True,
+                stop=True,
+            )
+
+        for i in range(SEQUENCES):
+            result = held.tile([P, TOKENS], F32, name=f"result{i}")
+            nc.scalar.activation(result[:], window_tiles[i][:], TANH, bias=bias[:])
+            nc.sync.dma_start(out[i], result[:])

@@ -11,6 +11,9 @@ ENTRIES = 192
 PIECE = ENTRIES // SEQUENCES
 PIECE_COLUMNS = PIECE // 16
 
+STRIP = 32
+STRIP_TOKENS = 96
+
 WARMING_MATMULS = 2
 
 FLOPS = 2 * P * P * ENTRIES
@@ -24,13 +27,13 @@ def tile_scatter_matmul_kernel(tc, base, x, w, b, offs, out):
     ):
         base_tiles = [held.tile([P, TOKENS], BF16, name=f"base{i}") for i in range(SEQUENCES)]
         nc.sync.dma_start(base_tiles[0][:], base[0])
-        nc.sync.dma_start(base_tiles[1][:], base[1])
         offsets = held.tile([P, ENTRIES // 16], U16, name="offsets")
         nc.sync.dma_start(offsets[:], offs)
         weights = held.tile([P, P], BF16, name="weights")
         nc.sync.dma_start(weights[:], w)
         picked = held.tile([P, ENTRIES], BF16, name="picked")
         nc.sync.dma_start(picked[:], x)
+        nc.sync.dma_start(base_tiles[1][:], base[1])
         bias = held.tile([P, 1], F32, name="bias")
         nc.sync.dma_start(bias[:], b)
 
@@ -49,9 +52,20 @@ def tile_scatter_matmul_kernel(tc, base, x, w, b, offs, out):
 
         window_tiles = [windows.tile([P, TOKENS], F32, name=f"window{i}") for i in range(SEQUENCES)]
         for i in range(SEQUENCES):
-            nc.tensor.matmul(window_tiles[i][:], identity[:], base_tiles[i][:], start=True, stop=True)
-
-        for i in range(SEQUENCES):
+            if i == 0:
+                nc.tensor.matmul(window_tiles[i][:], identity[:], base_tiles[i][:], start=True, stop=True)
+            else:
+                for token in range(0, TOKENS, STRIP_TOKENS):
+                    tokens = slice(token, min(token + STRIP_TOKENS, TOKENS))
+                    for feature in range(0, P, STRIP):
+                        features = slice(feature, feature + STRIP)
+                        nc.tensor.matmul(
+                            window_tiles[i][features, tokens],
+                            identity[:, features],
+                            base_tiles[i][:, tokens],
+                            start=True,
+                            stop=True,
+                        )
             piece = offsets[:, i * PIECE_COLUMNS : (i + 1) * PIECE_COLUMNS]
             nc.tensor.matmul(
                 window_tiles[i][:].indirect(piece),

@@ -11,8 +11,7 @@ ENTRIES = 192
 PIECE = ENTRIES // SEQUENCES
 PIECE_COLUMNS = PIECE // 16
 
-STRIP = 32
-STRIP_TOKENS = 96
+PIECE_TOKENS = 22
 
 WARMING_MATMULS = 2
 
@@ -55,17 +54,11 @@ def tile_scatter_matmul_kernel(tc, base, x, w, b, offs, out):
             if i == 0:
                 nc.tensor.matmul(window_tiles[i][:], identity[:], base_tiles[i][:], start=True, stop=True)
             else:
-                for token in range(0, TOKENS, STRIP_TOKENS):
-                    tokens = slice(token, min(token + STRIP_TOKENS, TOKENS))
-                    for feature in range(0, P, STRIP):
-                        features = slice(feature, feature + STRIP)
-                        nc.tensor.matmul(
-                            window_tiles[i][features, tokens],
-                            identity[:, features],
-                            base_tiles[i][:, tokens],
-                            start=True,
-                            stop=True,
-                        )
+                for token in range(0, TOKENS, PIECE_TOKENS):
+                    tokens = slice(token, min(token + PIECE_TOKENS, TOKENS))
+                    nc.tensor.matmul(
+                        window_tiles[i][:, tokens], identity[:], base_tiles[i][:, tokens], start=True, stop=True
+                    )
             piece = offsets[:, i * PIECE_COLUMNS : (i + 1) * PIECE_COLUMNS]
             nc.tensor.matmul(
                 window_tiles[i][:].indirect(piece),

import concourse.mybir as mybir
from concourse.masks import make_identity

BF16, F32, U16 = mybir.dt.bfloat16, mybir.dt.float32, mybir.dt.uint16
TANH = mybir.ActivationFunctionType.Tanh

P = 128
SEQUENCES = 2
TOKENS = 512
ENTRIES = 192
PIECE = ENTRIES // SEQUENCES
PIECE_COLUMNS = PIECE // 16

PIECE_TOKENS = 22

WARMING_MATMULS = 2

FLOPS = 2 * P * P * ENTRIES


def tile_scatter_matmul_kernel(tc, base, x, w, b, offs, out):
    nc = tc.nc
    with (
        tc.tile_pool(name="held", bufs=1) as held,
        tc.psum_pool(name="windows", bufs=1) as windows,
    ):
        base_tiles = [held.tile([P, TOKENS], BF16, name=f"base{i}") for i in range(SEQUENCES)]
        nc.sync.dma_start(base_tiles[0][:], base[0])
        offsets = held.tile([P, ENTRIES // 16], U16, name="offsets")
        nc.sync.dma_start(offsets[:], offs)
        weights = held.tile([P, P], BF16, name="weights")
        nc.sync.dma_start(weights[:], w)
        picked = held.tile([P, ENTRIES], BF16, name="picked")
        nc.sync.dma_start(picked[:], x)
        nc.sync.dma_start(base_tiles[1][:], base[1])
        bias = held.tile([P, 1], F32, name="bias")
        nc.sync.dma_start(bias[:], b)

        zeros = held.tile([P, TOKENS], BF16, name="zeros")
        nc.vector.memset(zeros[:], 0.0)
        idle_product = windows.tile([P, TOKENS], F32, name="idle_product")
        for turn in range(WARMING_MATMULS):
            nc.tensor.matmul(idle_product[:], zeros[:, 0:P], zeros[:], start=True, stop=True)

        warm = held.tile([P, 1], F32, name="warm")
        nc.vector.memset(warm[:], 0.0)
        nc.scalar.activation(warm[:], warm[:], TANH)

        identity = held.tile([P, P], BF16, name="identity")
        make_identity(nc, identity[:])

        window_tiles = [windows.tile([P, TOKENS], F32, name=f"window{i}") for i in range(SEQUENCES)]
        for i in range(SEQUENCES):
            if i == 0:
                nc.tensor.matmul(window_tiles[i][:], identity[:], base_tiles[i][:], start=True, stop=True)
            else:
                for token in range(0, TOKENS, PIECE_TOKENS):
                    tokens = slice(token, min(token + PIECE_TOKENS, TOKENS))
                    nc.tensor.matmul(
                        window_tiles[i][:, tokens], identity[:], base_tiles[i][:, tokens], start=True, stop=True
                    )
            piece = offsets[:, i * PIECE_COLUMNS : (i + 1) * PIECE_COLUMNS]
            nc.tensor.matmul(
                window_tiles[i][:].indirect(piece),
                weights[:],
                picked[:, i * PIECE : (i + 1) * PIECE],
                start=True,
                stop=True,
            )

        for i in range(SEQUENCES):
            result = held.tile([P, TOKENS], F32, name=f"result{i}")
            nc.scalar.activation(result[:], window_tiles[i][:], TANH, bias=bias[:])
            nc.sync.dma_start(out[i], result[:])
